import numpy as np
import ml_dtypes


def mxq(x, axis, fmt="e4m3"):
    dtype, down = {"e4m3": (ml_dtypes.float8_e4m3fn, 7), "e5m2": (ml_dtypes.float8_e5m2, 14)}[fmt]
    v = np.moveaxis(np.asarray(x, np.float32).astype(ml_dtypes.bfloat16).astype(np.float64), axis, -1)
    blocks = v.reshape(v.shape[:-1] + (-1, 32))
    amax = np.abs(blocks).max(-1, keepdims=True)
    byte = np.maximum(np.where(amax > 0, np.frexp(amax)[1] - 1 + 127, 0) - down, 1)
    scale = np.exp2(byte - 127.0)
    codes = (blocks / scale).astype(np.float32).astype(dtype).astype(np.float64)
    return np.moveaxis((codes * scale).reshape(v.shape), -1, axis)


WIDE = False


def mx_kscale(k):
    if not WIDE:
        return np.ones(k)
    levels = np.array([10, -10, 5, -5, 0])
    if k % 512:
        return np.exp2(np.random.permutation(np.resize(levels, k // 32))).repeat(32)
    a = np.empty((k // 512, 16))
    for p in range(k // 512):
        a[p, :8] = np.random.permutation(np.resize(levels, 8))
        for g in range(8):
            far = levels[np.abs(levels - a[p, g]) >= 10]
            a[p, g + 8] = far[np.random.randint(len(far))]
    return np.exp2(a.ravel()).repeat(32)


def f64(x):
    return np.asarray(x).astype(np.float64)


def striped(idx):
    return np.tile(idx.reshape(-1, 16).T, (8, 1)).astype(np.uint16)


def unstriped(offs):
    return offs[:16].T.reshape(-1).astype(np.int64)


K, T, E, C, N = 1024, 1024, 2, 256, 256


def by_expert(wq, xq):
    return np.concatenate([wq[e].T @ xq[:, e * C:(e + 1) * C] for e in range(E)], axis=1)


def setup_inputs():
    n = np.random.standard_normal
    s = mx_kscale(K)[:, None]
    return {
        "xT": (n((K, T)) * s).astype(np.float32),
        "w": (n((E, K, N)) / np.sqrt(K) / s[None]).astype(np.float32),
        "gate": np.tile(np.random.uniform(0.2, 1.0, E * C), (N, 1)).astype(np.float32),
        "offs": striped(np.random.permutation(T)[:E * C]),
    }


def reference(xT, w, gate, offs):
    idx = unstriped(offs)
    xq = mxq(f64(xT)[:, idx], 0, "e4m3")
    y = by_expert(mxq(f64(w), 1, "e4m3"), xq)
    out = np.zeros((N, T))
    out[:, idx] = f64(gate) * y
    return out

@@ -1,0 +1,173 @@
+from contextlib import ExitStack
+
+import concourse.mybir as mybir
+
+K, T, E, C, N = 1024, 1024, 2, 256, 256
+FLOPS = 2 * K * N * E * C
+
+F32 = mybir.dt.float32
+BF16 = mybir.dt.bfloat16
+U32 = mybir.dt.uint32
+U16 = mybir.dt.uint16
+U8 = mybir.dt.uint8
+FP8X4 = mybir.dt.float8_e4m3fn_x4
+MULT = mybir.AluOpType.mult
+
+P = 128
+PACK = 4
+PASSES = K // (P * PACK)
+FB = N // P
+LCOLS = C // 16
+
+
+def tile_routed_moe_kernel(tc, xT, w, gate, offs, out):
+    nc = tc.nc
+    with ExitStack() as ctx:
+        lists = ctx.enter_context(tc.tile_pool(name="lists", bufs=1))
+        keep = ctx.enter_context(tc.tile_pool(name="keep", bufs=1))
+        psum = ctx.enter_context(tc.psum_pool(name="psum", bufs=1))
+
+        offsets = lists.tile([P, E * C // 16], U16, name="offsets")
+        nc.sync.dma_start(offsets[:], offs)
+
+        x_view = xT.rearrange("(g p t) n -> g p t n", p=P, t=PACK)
+        w_view = w.rearrange("e (g p j) n -> e g p j n", p=P, j=PACK)
+
+        plane = {}
+        for g in range(PASSES):
+            for t in range(PACK):
+                plane[g, t] = keep.tile([P, T], F32, name="plane%d%d" % (g, t))
+                nc.sync.dma_start(out=plane[g, t][:], in_=x_view[g, :, t, :])
+
+        w_raw = {}
+        gate_sb = {}
+
+        def load_w(e):
+            for g in range(PASSES):
+                w_raw[e, g] = keep.tile([P, PACK, N], F32, name="wraw%d%d" % (e, g))
+                nc.sync.dma_start(out=w_raw[e, g][:], in_=w_view[e, g])
+
+        load_w(0)
+        for fb in range(FB):
+            gate_sb[fb] = keep.tile([P, E * C], F32, name="gate%d" % fb)
+            nc.sync.dma_start(out=gate_sb[fb][:], in_=gate[fb * P:(fb + 1) * P, :])
+        load_w(1)
+
+        window = {}
+        for fb in range(FB):
+            window[fb] = keep.tile([P, T], F32, name="window%d" % fb)
+            nc.vector.memset(window[fb][:], 0.0)
+
+        def slots(e):
+            return offsets[:, e * LCOLS:(e + 1) * LCOLS]
+
+        picked = {}
+        x_grouped = {}
+        x_codes = {}
+        x_scales = {}
+        for g in range(PASSES):
+            for e in range(E):
+                picked[g, e] = keep.tile([P, PACK, C], F32, name="picked%d%d" % (g, e))
+                x_grouped[g, e] = keep.tile([P, C, PACK], BF16, name="xgrp%d%d" % (g, e), align_bytes=64)
+                x_codes[g, e] = keep.tile([P, C], U32, name="xcodes%d%d" % (g, e), align_bytes=64)
+                x_scales[g, e] = keep.tile([P, C], U8, name="xscales%d%d" % (g, e), align_bytes=64)
+
+        def gather(g, e, t):
+            nc.vector.tensor_copy(picked[g, e][:, t, :], plane[g, t][:].indirect(slots(e)))
+
+        def group_x(g, e):
+            nc.scalar.copy(out=x_grouped[g, e][:], in_=picked[g, e][:].rearrange("p t n -> p n t"))
+
+        def quant_x(g, e):
+            nc.vector.quantize_mx(
+                out=x_codes[g, e][:].bitcast(FP8X4),
+                scales=x_scales[g, e][:],
+                in_=x_grouped[g, e][:].rearrange("p n t -> p (n t)"),
+            )
+
+        w_grouped = {}
+        w_codes = {}
+        w_scales = {}
+        acc = {}
+        sums = {}
+        for e in range(E):
+            for fb in range(FB):
+                w_grouped[e, fb] = keep.tile([P, PASSES, P, PACK], BF16, name="wgrp%d%d" % (e, fb), align_bytes=64)
+                w_codes[e, fb] = keep.tile([P, PASSES * P], U32, name="wcodes%d%d" % (e, fb), align_bytes=64)
+                w_scales[e, fb] = keep.tile([P, PASSES * P], U8, name="wscales%d%d" % (e, fb), align_bytes=64)
+                acc[e, fb] = psum.tile([P, C], F32, name="acc%d%d" % (e, fb))
+                sums[e, fb] = keep.tile([P, C], F32, name="sums%d%d" % (e, fb))
+
+        def group_w(e, fb):
+            for g in range(PASSES):
+                nc.scalar.copy(
+                    out=w_grouped[e, fb][:, g, :, :],
+                    in_=w_raw[e, g][:, :, fb * P:(fb + 1) * P].rearrange("p j n -> p n j"),
+                )
+
+        def quant_w(e, fb):
+            nc.vector.quantize_mx(
+                out=w_codes[e, fb][:].bitcast(FP8X4),
+                scales=w_scales[e, fb][:],
+                in_=w_grouped[e, fb][:].rearrange("p g n j -> p (g n j)"),
+            )
+
+        def multiply(e, fb):
+            for g in range(PASSES):
+                cols = slice(g * P, (g + 1) * P)
+                nc.tensor.matmul_mx(
+                    out=acc[e, fb][:],
+                    lhsT=w_codes[e, fb][:, cols].bitcast(FP8X4),
+                    lhsT_scale=w_scales[e, fb][:, cols],
+                    rhs=x_codes[g, e][:].bitcast(FP8X4),
+                    rhs_scale=x_scales[g, e][:],
+                    start=(g == 0),
+                    stop=(g == PASSES - 1),
+                )
+            nc.scalar.copy(out=sums[e, fb][:], in_=acc[e, fb][:])
+
+        def scatter(e, fb):
+            nc.vector.tensor_tensor(
+                window[fb][:].indirect(slots(e)),
+                sums[e, fb][:],
+                gate_sb[fb][:, e * C:(e + 1) * C],
+                MULT,
+            )
+
+        for t in range(PACK):
+            gather(0, 0, t)
+            gather(0, 1, t)
+        group_x(0, 0)
+        group_x(0, 1)
+        gather(1, 0, 0)
+        quant_x(0, 0)
+        gather(1, 0, 1)
+        quant_x(0, 1)
+        gather(1, 0, 2)
+        gather(1, 0, 3)
+        group_x(1, 0)
+        gather(1, 1, 0)
+        gather(1, 1, 1)
+        quant_x(1, 0)
+        gather(1, 1, 2)
+        gather(1, 1, 3)
+        group_w(0, 0)
+        quant_w(0, 0)
+        multiply(0, 0)
+        group_w(0, 1)
+        group_x(1, 1)
+        quant_w(0, 1)
+        scatter(0, 0)
+        multiply(0, 1)
+        quant_x(1, 1)
+        group_w(1, 0)
+        quant_w(1, 0)
+        scatter(0, 1)
+        multiply(1, 0)
+        group_w(1, 1)
+        quant_w(1, 1)
+        scatter(1, 0)
+        nc.sync.dma_start(out=out[0:P, :], in_=window[0][:])
+        multiply(1, 1)
+        scatter(1, 1)
+        nc.sync.dma_start(out=out[P:2 * P, :], in_=window[1][:])

@@ -18,6 +18,7 @@ PACK = 4
 PASSES = K // (P * PACK)
 FB = N // P
 LCOLS = C // 16
+HALF = T // 2
 
 
 def tile_routed_moe_kernel(tc, xT, w, gate, offs, out):
@@ -33,56 +34,61 @@ def tile_routed_moe_kernel(tc, xT, w, gate, offs, out):
         x_view = xT.rearrange("(g p t) n -> g p t n", p=P, t=PACK)
         w_view = w.rearrange("e (g p j) n -> e g p j n", p=P, j=PACK)
 
-        plane = {}
+        raw = {}
         for g in range(PASSES):
-            for t in range(PACK):
-                plane[g, t] = keep.tile([P, T], F32, name="plane%d%d" % (g, t))
-                nc.sync.dma_start(out=plane[g, t][:], in_=x_view[g, :, t, :])
-
+            raw[g] = keep.tile([P, PACK, T], F32, name="raw%d" % g)
         w_raw = {}
         gate_sb = {}
 
-        def load_w(e):
-            for g in range(PASSES):
-                w_raw[e, g] = keep.tile([P, PACK, N], F32, name="wraw%d%d" % (e, g))
-                nc.sync.dma_start(out=w_raw[e, g][:], in_=w_view[e, g])
+        def load_x(g, t):
+            nc.sync.dma_start(out=raw[g][:, t, :], in_=x_view[g, :, t, :])
 
-        load_w(0)
-        for fb in range(FB):
+        def load_w(e, g):
+            w_raw[e, g] = keep.tile([P, PACK, N], F32, name="wraw%d%d" % (e, g))
+            nc.sync.dma_start(out=w_raw[e, g][:], in_=w_view[e, g])
+
+        def load_gate(fb):
             gate_sb[fb] = keep.tile([P, E * C], F32, name="gate%d" % fb)
             nc.sync.dma_start(out=gate_sb[fb][:], in_=gate[fb * P:(fb + 1) * P, :])
-        load_w(1)
+
+        for t in range(PACK):
+            load_x(0, t)
+        load_x(1, 0)
+        load_x(1, 1)
+        load_w(0, 0)
+        load_x(1, 2)
+        load_w(0, 1)
+        load_x(1, 3)
+        load_w(1, 0)
+        load_gate(0)
+        load_w(1, 1)
+        load_gate(1)
 
         window = {}
         for fb in range(FB):
             window[fb] = keep.tile([P, T], F32, name="window%d" % fb)
             nc.vector.memset(window[fb][:], 0.0)
 
-        def slots(e):
-            return offsets[:, e * LCOLS:(e + 1) * LCOLS]
-
-        picked = {}
         x_grouped = {}
         x_codes = {}
         x_scales = {}
         for g in range(PASSES):
-            for e in range(E):
-                picked[g, e] = keep.tile([P, PACK, C], F32, name="picked%d%d" % (g, e))
-                x_grouped[g, e] = keep.tile([P, C, PACK], BF16, name="xgrp%d%d" % (g, e), align_bytes=64)
-                x_codes[g, e] = keep.tile([P, C], U32, name="xcodes%d%d" % (g, e), align_bytes=64)
-                x_scales[g, e] = keep.tile([P, C], U8, name="xscales%d%d" % (g, e), align_bytes=64)
+            x_grouped[g] = keep.tile([P, E * C, PACK], BF16, name="xgrp%d" % g, align_bytes=64)
+            x_codes[g] = keep.tile([P, E * C], U32, name="xcodes%d" % g, align_bytes=64)
+            x_scales[g] = keep.tile([P, E * C], U8, name="xscales%d" % g, align_bytes=64)
 
-        def gather(g, e, t):
-            nc.vector.tensor_copy(picked[g, e][:, t, :], plane[g, t][:].indirect(slots(e)))
+        def gather(g, t, first, count):
+            nc.vector.tensor_copy(
+                x_grouped[g][:, first * C:(first + count) * C, t],
+                raw[g][:, t, :].indirect(offsets[:, first * LCOLS:(first + count) * LCOLS]),
+            )
 
-        def group_x(g, e):
-            nc.scalar.copy(out=x_grouped[g, e][:], in_=picked[g, e][:].rearrange("p t n -> p n t"))
-
-        def quant_x(g, e):
+        def quant_x(g, first, count):
+            cols = slice(first * C, (first + count) * C)
             nc.vector.quantize_mx(
-                out=x_codes[g, e][:].bitcast(FP8X4),
-                scales=x_scales[g, e][:],
-                in_=x_grouped[g, e][:].rearrange("p n t -> p (n t)"),
+                out=x_codes[g][:, cols].bitcast(FP8X4),
+                scales=x_scales[g][:, cols],
+                in_=x_grouped[g][:, cols, :].rearrange("p n t -> p (n t)"),
             )
 
         w_grouped = {}
@@ -91,83 +97,84 @@ def tile_routed_moe_kernel(tc, xT, w, gate, offs, out):
         acc = {}
         sums = {}
         for e in range(E):
+            w_grouped[e] = keep.tile([P, FB, PASSES, P, PACK], BF16, name="wgrp%d" % e, align_bytes=64)
+            w_codes[e] = keep.tile([P, FB * PASSES * P], U32, name="wcodes%d" % e, align_bytes=64)
+            w_scales[e] = keep.tile([P, FB * PASSES * P], U8, name="wscales%d" % e, align_bytes=64)
             for fb in range(FB):
-                w_grouped[e, fb] = keep.tile([P, PASSES, P, PACK], BF16, name="wgrp%d%d" % (e, fb), align_bytes=64)
-                w_codes[e, fb] = keep.tile([P, PASSES * P], U32, name="wcodes%d%d" % (e, fb), align_bytes=64)
-                w_scales[e, fb] = keep.tile([P, PASSES * P], U8, name="wscales%d%d" % (e, fb), align_bytes=64)
                 acc[e, fb] = psum.tile([P, C], F32, name="acc%d%d" % (e, fb))
                 sums[e, fb] = keep.tile([P, C], F32, name="sums%d%d" % (e, fb))
 
-        def group_w(e, fb):
-            for g in range(PASSES):
-                nc.scalar.copy(
-                    out=w_grouped[e, fb][:, g, :, :],
-                    in_=w_raw[e, g][:, :, fb * P:(fb + 1) * P].rearrange("p j n -> p n j"),
-                )
+        def group_w(e, g):
+            nc.scalar.copy(
+                out=w_grouped[e][:, :, g, :, :],
+                in_=w_raw[e, g][:].rearrange("p j (f n) -> p f n j", f=FB),
+            )
 
-        def quant_w(e, fb):
+        def quant_w(e, first, count):
+            cols = slice(first * PASSES * P, (first + count) * PASSES * P)
             nc.vector.quantize_mx(
-                out=w_codes[e, fb][:].bitcast(FP8X4),
-                scales=w_scales[e, fb][:],
-                in_=w_grouped[e, fb][:].rearrange("p g n j -> p (g n j)"),
+                out=w_codes[e][:, cols].bitcast(FP8X4),
+                scales=w_scales[e][:, cols],
+                in_=w_grouped[e][:, first:first + count, :, :, :].rearrange("p f g n j -> p (f g n j)"),
             )
 
         def multiply(e, fb):
             for g in range(PASSES):
-                cols = slice(g * P, (g + 1) * P)
+                wcols = slice((fb * PASSES + g) * P, (fb * PASSES + g + 1) * P)
+                xcols = slice(e * C, (e + 1) * C)
                 nc.tensor.matmul_mx(
                     out=acc[e, fb][:],
-                    lhsT=w_codes[e, fb][:, cols].bitcast(FP8X4),
-                    lhsT_scale=w_scales[e, fb][:, cols],
-                    rhs=x_codes[g, e][:].bitcast(FP8X4),
-                    rhs_scale=x_scales[g, e][:],
+                    lhsT=w_codes[e][:, wcols].bitcast(FP8X4),
+                    lhsT_scale=w_scales[e][:, wcols],
+                    rhs=x_codes[g][:, xcols].bitcast(FP8X4),
+                    rhs_scale=x_scales[g][:, xcols],
                     start=(g == 0),
                     stop=(g == PASSES - 1),
                 )
+
+        def unload(e, fb):
             nc.scalar.copy(out=sums[e, fb][:], in_=acc[e, fb][:])
 
         def scatter(e, fb):
             nc.vector.tensor_tensor(
-                window[fb][:].indirect(slots(e)),
+                window[fb][:].indirect(offsets[:, e * LCOLS:(e + 1) * LCOLS]),
                 sums[e, fb][:],
                 gate_sb[fb][:, e * C:(e + 1) * C],
                 MULT,
             )
 
+        def store(fb):
+            nc.sync.dma_start(out=out[fb * P:(fb + 1) * P, :], in_=window[fb][:])
+
         for t in range(PACK):
-            gather(0, 0, t)
-            gather(0, 1, t)
-        group_x(0, 0)
-        group_x(0, 1)
-        gather(1, 0, 0)
-        quant_x(0, 0)
-        gather(1, 0, 1)
-        quant_x(0, 1)
-        gather(1, 0, 2)
-        gather(1, 0, 3)
-        group_x(1, 0)
-        gather(1, 1, 0)
-        gather(1, 1, 1)
-        quant_x(1, 0)
-        gather(1, 1, 2)
-        gather(1, 1, 3)
+            gather(0, t, 0, 2)
+        gather(1, 0, 0, 2)
+        gather(1, 1, 0, 2)
         group_w(0, 0)
-        quant_w(0, 0)
-        multiply(0, 0)
+        quant_x(0, 0, 1)
+        gather(1, 2, 0, 2)
         group_w(0, 1)
-        group_x(1, 1)
-        quant_w(0, 1)
-        scatter(0, 0)
-        multiply(0, 1)
-        quant_x(1, 1)
+        quant_w(0, 0, 1)
+        gather(1, 3, 0, 1)
+        gather(1, 3, 1, 1)
         group_w(1, 0)
-        quant_w(1, 0)
-        scatter(0, 1)
-        multiply(1, 0)
+        quant_x(1, 0, 1)
+        multiply(0, 0)
+        unload(0, 0)
+        quant_x(0, 1, 1)
+        quant_w(0, 1, 1)
+        multiply(0, 1)
+        unload(0, 1)
+        quant_x(1, 1, 1)
+        scatter(0, 0)
         group_w(1, 1)
-        quant_w(1, 1)
-        scatter(1, 0)
-        nc.sync.dma_start(out=out[0:P, :], in_=window[0][:])
+        quant_w(1, 0, 2)
+        multiply(1, 0)
+        unload(1, 0)
         multiply(1, 1)
+        unload(1, 1)
+        scatter(0, 1)
+        scatter(1, 0)
+        store(0)
         scatter(1, 1)
-        nc.sync.dma_start(out=out[P:2 * P, :], in_=window[1][:])
+        store(1)

@@ -34,14 +34,18 @@ def tile_routed_moe_kernel(tc, xT, w, gate, offs, out):
         x_view = xT.rearrange("(g p t) n -> g p t n", p=P, t=PACK)
         w_view = w.rearrange("e (g p j) n -> e g p j n", p=P, j=PACK)
 
-        raw = {}
-        for g in range(PASSES):
-            raw[g] = keep.tile([P, PACK, T], F32, name="raw%d" % g)
+        raw = keep.tile([P, PACK, T], F32, name="raw")
+        plane = {}
+        for t in range(PACK):
+            plane[t] = keep.tile([P, 2 * T], F32, name="plane%d" % t)
         w_raw = {}
         gate_sb = {}
 
         def load_x(g, t):
-            nc.sync.dma_start(out=raw[g][:, t, :], in_=x_view[g, :, t, :])
+            if g == 0:
+                nc.sync.dma_start(out=plane[t][:, 0:T], in_=x_view[g, :, t, :])
+            else:
+                nc.sync.dma_start(out=raw[:, t, :], in_=x_view[g, :, t, :])
 
         def load_w(e, g):
             w_raw[e, g] = keep.tile([P, PACK, N], F32, name="wraw%d%d" % (e, g))
@@ -77,10 +81,19 @@ def tile_routed_moe_kernel(tc, xT, w, gate, offs, out):
             x_codes[g] = keep.tile([P, E * C], U32, name="xcodes%d" % g, align_bytes=64)
             x_scales[g] = keep.tile([P, E * C], U8, name="xscales%d" % g, align_bytes=64)
 
+        picked = keep.tile([P, PACK, E * C], F32, name="picked")
+
+        def gather_plain(t):
+            nc.vector.tensor_copy(picked[:, t, :], plane[t][:].indirect(offsets[:]))
+
+        def group_x(e):
+            cols = slice(e * C, (e + 1) * C)
+            nc.scalar.copy(out=x_grouped[0][:, cols, :], in_=picked[:, :, cols].rearrange("p t n -> p n t"))
+
         def gather(g, t, first, count):
             nc.vector.tensor_copy(
                 x_grouped[g][:, first * C:(first + count) * C, t],
-                raw[g][:, t, :].indirect(offsets[:, first * LCOLS:(first + count) * LCOLS]),
+                raw[:, t, :].indirect(offsets[:, first * LCOLS:(first + count) * LCOLS]),
             )
 
         def quant_x(g, first, count):
@@ -147,7 +160,8 @@ def tile_routed_moe_kernel(tc, xT, w, gate, offs, out):
             nc.sync.dma_start(out=out[fb * P:(fb + 1) * P, :], in_=window[fb][:])
 
         for t in range(PACK):
-            gather(0, t, 0, 2)
+            gather_plain(t)
+        group_x(0)
         gather(1, 0, 0, 2)
         gather(1, 1, 0, 2)
         group_w(0, 0)
@@ -157,14 +171,15 @@ def tile_routed_moe_kernel(tc, xT, w, gate, offs, out):
         quant_w(0, 0, 1)
         gather(1, 3, 0, 1)
         gather(1, 3, 1, 1)
+        group_x(1)
         group_w(1, 0)
         quant_x(1, 0, 1)
         multiply(0, 0)
         unload(0, 0)
-        quant_x(0, 1, 1)
         quant_w(0, 1, 1)
         multiply(0, 1)
         unload(0, 1)
+        quant_x(0, 1, 1)
         quant_x(1, 1, 1)
         scatter(0, 0)
         group_w(1, 1)

@@ -34,18 +34,13 @@ def tile_routed_moe_kernel(tc, xT, w, gate, offs, out):
         x_view = xT.rearrange("(g p t) n -> g p t n", p=P, t=PACK)
         w_view = w.rearrange("e (g p j) n -> e g p j n", p=P, j=PACK)
 
-        raw = keep.tile([P, PACK, T], F32, name="raw")
         plane = {}
-        for t in range(PACK):
-            plane[t] = keep.tile([P, 2 * T], F32, name="plane%d" % t)
         w_raw = {}
         gate_sb = {}
 
         def load_x(g, t):
-            if g == 0:
-                nc.sync.dma_start(out=plane[t][:, 0:T], in_=x_view[g, :, t, :])
-            else:
-                nc.sync.dma_start(out=raw[:, t, :], in_=x_view[g, :, t, :])
+            plane[g, t] = keep.tile([P, 2 * T], F32, name="plane%d%d" % (g, t))
+            nc.sync.dma_start(out=plane[g, t][:, 0:T], in_=x_view[g, :, t, :])
 
         def load_w(e, g):
             w_raw[e, g] = keep.tile([P, PACK, N], F32, name="wraw%d%d" % (e, g))
@@ -55,8 +50,10 @@ def tile_routed_moe_kernel(tc, xT, w, gate, offs, out):
             gate_sb[fb] = keep.tile([P, E * C], F32, name="gate%d" % fb)
             nc.sync.dma_start(out=gate_sb[fb][:], in_=gate[fb * P:(fb + 1) * P, :])
 
-        for t in range(PACK):
-            load_x(0, t)
+        load_x(0, 0)
+        load_x(0, 1)
+        load_x(0, 2)
+        load_x(0, 3)
         load_x(1, 0)
         load_x(1, 1)
         load_w(0, 0)
@@ -73,28 +70,33 @@ def tile_routed_moe_kernel(tc, xT, w, gate, offs, out):
             window[fb] = keep.tile([P, T], F32, name="window%d" % fb)
             nc.vector.memset(window[fb][:], 0.0)
 
+        picked = {}
         x_grouped = {}
         x_codes = {}
         x_scales = {}
         for g in range(PASSES):
+            picked[g] = keep.tile([P, PACK, E * C], F32, name="picked%d" % g)
             x_grouped[g] = keep.tile([P, E * C, PACK], BF16, name="xgrp%d" % g, align_bytes=64)
             x_codes[g] = keep.tile([P, E * C], U32, name="xcodes%d" % g, align_bytes=64)
             x_scales[g] = keep.tile([P, E * C], U8, name="xscales%d" % g, align_bytes=64)
 
-        picked = keep.tile([P, PACK, E * C], F32, name="picked")
-
-        def gather_plain(t):
-            nc.vector.tensor_copy(picked[:, t, :], plane[t][:].indirect(offsets[:]))
-
-        def group_x(e):
-            cols = slice(e * C, (e + 1) * C)
-            nc.scalar.copy(out=x_grouped[0][:, cols, :], in_=picked[:, :, cols].rearrange("p t n -> p n t"))
-
         def gather(g, t, first, count):
             nc.vector.tensor_copy(
-                x_grouped[g][:, first * C:(first + count) * C, t],
-                raw[:, t, :].indirect(offsets[:, first * LCOLS:(first + count) * LCOLS]),
+                picked[g][:, t, first * C:(first + count) * C],
+                plane[g, t][:].indirect(offsets[:, first * LCOLS:(first + count) * LCOLS]),
             )
+
+        def interleave(engine, dst, src):
+            dst4 = dst.rearrange("p (c i) t -> p c t i", i=4)
+            src4 = src.rearrange("p t (c i) -> p c t i", i=4)
+            if engine == "S":
+                nc.scalar.copy(out=dst4, in_=src4)
+            else:
+                nc.vector.tensor_copy(out=dst4, in_=src4)
+
+        def group_x(g, first, count, engine):
+            cols = slice(first * C, (first + count) * C)
+            interleave(engine, x_grouped[g][:, cols, :], picked[g][:, :, cols])
 
         def quant_x(g, first, count):
             cols = slice(first * C, (first + count) * C)
@@ -110,30 +112,27 @@ def tile_routed_moe_kernel(tc, xT, w, gate, offs, out):
         acc = {}
         sums = {}
         for e in range(E):
-            w_grouped[e] = keep.tile([P, FB, PASSES, P, PACK], BF16, name="wgrp%d" % e, align_bytes=64)
-            w_codes[e] = keep.tile([P, FB * PASSES * P], U32, name="wcodes%d" % e, align_bytes=64)
-            w_scales[e] = keep.tile([P, FB * PASSES * P], U8, name="wscales%d" % e, align_bytes=64)
+            w_grouped[e] = keep.tile([P, PASSES, N, PACK], BF16, name="wgrp%d" % e, align_bytes=64)
+            w_codes[e] = keep.tile([P, PASSES * N], U32, name="wcodes%d" % e, align_bytes=64)
+            w_scales[e] = keep.tile([P, PASSES * N], U8, name="wscales%d" % e, align_bytes=64)
             for fb in range(FB):
                 acc[e, fb] = psum.tile([P, C], F32, name="acc%d%d" % (e, fb))
                 sums[e, fb] = keep.tile([P, C], F32, name="sums%d%d" % (e, fb))
 
-        def group_w(e, g):
-            nc.scalar.copy(
-                out=w_grouped[e][:, :, g, :, :],
-                in_=w_raw[e, g][:].rearrange("p j (f n) -> p f n j", f=FB),
-            )
+        def group_w(e, g, engine):
+            interleave(engine, w_grouped[e][:, g, :, :], w_raw[e, g][:])
 
         def quant_w(e, first, count):
-            cols = slice(first * PASSES * P, (first + count) * PASSES * P)
+            cols = slice(first * N, (first + count) * N)
             nc.vector.quantize_mx(
                 out=w_codes[e][:, cols].bitcast(FP8X4),
                 scales=w_scales[e][:, cols],
-                in_=w_grouped[e][:, first:first + count, :, :, :].rearrange("p f g n j -> p (f g n j)"),
+                in_=w_grouped[e][:, first:first + count, :, :].rearrange("p g n j -> p (g n j)"),
             )
 
         def multiply(e, fb):
             for g in range(PASSES):
-                wcols = slice((fb * PASSES + g) * P, (fb * PASSES + g + 1) * P)
+                wcols = slice(g * N + fb * P, g * N + (fb + 1) * P)
                 xcols = slice(e * C, (e + 1) * C)
                 nc.tensor.matmul_mx(
                     out=acc[e, fb][:],
@@ -159,36 +158,39 @@ def tile_routed_moe_kernel(tc, xT, w, gate, offs, out):
         def store(fb):
             nc.sync.dma_start(out=out[fb * P:(fb + 1) * P, :], in_=window[fb][:])
 
-        for t in range(PACK):
-            gather_plain(t)
-        group_x(0)
+        gather(0, 0, 0, 2)
+        gather(0, 1, 0, 2)
+        gather(0, 2, 0, 2)
+        gather(0, 3, 0, 2)
         gather(1, 0, 0, 2)
+        group_x(0, 0, 2, "S")
         gather(1, 1, 0, 2)
-        group_w(0, 0)
+        group_w(0, 0, "S")
         quant_x(0, 0, 1)
         gather(1, 2, 0, 2)
-        group_w(0, 1)
         quant_w(0, 0, 1)
-        gather(1, 3, 0, 1)
-        gather(1, 3, 1, 1)
-        group_x(1)
-        group_w(1, 0)
+        group_w(0, 1, "S")
+        gather(1, 3, 0, 2)
+        group_w(1, 0, "S")
+        group_x(1, 0, 1, "V")
+        quant_w(0, 1, 1)
         quant_x(1, 0, 1)
         multiply(0, 0)
-        unload(0, 0)
-        quant_w(0, 1, 1)
         multiply(0, 1)
-        unload(0, 1)
+        group_x(1, 1, 1, "S")
         quant_x(0, 1, 1)
+        unload(0, 0)
+        quant_w(1, 0, 1)
         quant_x(1, 1, 1)
+        group_w(1, 1, "S")
         scatter(0, 0)
-        group_w(1, 1)
-        quant_w(1, 0, 2)
+        unload(0, 1)
+        quant_w(1, 1, 1)
+        scatter(0, 1)
         multiply(1, 0)
         unload(1, 0)
         multiply(1, 1)
         unload(1, 1)
-        scatter(0, 1)
         scatter(1, 0)
         store(0)
         scatter(1, 1)

@@ -172,7 +172,7 @@ def tile_routed_moe_kernel(tc, xT, w, gate, offs, out):
         group_w(0, 1, "S")
         gather(1, 3, 0, 2)
         group_w(1, 0, "S")
-        group_x(1, 0, 1, "V")
+        group_x(1, 0, 1, "S")
         quant_w(0, 1, 1)
         quant_x(1, 0, 1)
         multiply(0, 0)

@@ -12,13 +12,13 @@ U16 = mybir.dt.uint16
 U8 = mybir.dt.uint8
 FP8X4 = mybir.dt.float8_e4m3fn_x4
 MULT = mybir.AluOpType.mult
+COPY = mybir.ActivationFunctionType.Copy
 
 P = 128
 PACK = 4
 PASSES = K // (P * PACK)
 FB = N // P
 LCOLS = C // 16
-HALF = T // 2
 
 
 def tile_routed_moe_kernel(tc, xT, w, gate, offs, out):
@@ -35,12 +35,17 @@ def tile_routed_moe_kernel(tc, xT, w, gate, offs, out):
         w_view = w.rearrange("e (g p j) n -> e g p j n", p=P, j=PACK)
 
         plane = {}
+        plane_bf = {}
         w_raw = {}
         gate_sb = {}
 
         def load_x(g, t):
             plane[g, t] = keep.tile([P, 2 * T], F32, name="plane%d%d" % (g, t))
             nc.sync.dma_start(out=plane[g, t][:, 0:T], in_=x_view[g, :, t, :])
+
+        def load_xb(g, t):
+            plane[g, t] = keep.tile([P, T], F32, name="plane%d%d" % (g, t))
+            nc.sync.dma_start(out=plane[g, t][:], in_=x_view[g, :, t, :])
 
         def load_w(e, g):
             w_raw[e, g] = keep.tile([P, PACK, N], F32, name="wraw%d%d" % (e, g))
@@ -80,23 +85,39 @@ def tile_routed_moe_kernel(tc, xT, w, gate, offs, out):
             x_codes[g] = keep.tile([P, E * C], U32, name="xcodes%d" % g, align_bytes=64)
             x_scales[g] = keep.tile([P, E * C], U8, name="xscales%d" % g, align_bytes=64)
 
+        def copy_on(engine, dst, src):
+            if engine == "S":
+                nc.scalar.copy(out=dst, in_=src)
+            elif engine == "G":
+                nc.gpsimd.tensor_copy(out=dst, in_=src)
+            else:
+                nc.vector.tensor_copy(out=dst, in_=src)
+
         def gather(g, t, first, count):
             nc.vector.tensor_copy(
                 picked[g][:, t, first * C:(first + count) * C],
                 plane[g, t][:].indirect(offsets[:, first * LCOLS:(first + count) * LCOLS]),
             )
 
+        def cast_plane(g, t, engine):
+            plane_bf[g, t] = keep.tile([P, T], BF16, name="planebf%d%d" % (g, t))
+            copy_on(engine, plane_bf[g, t][:], plane[g, t][:])
+
+        def gather_s(g, t, first, count):
+            nc.scalar.activation(
+                x_grouped[g][:, first * C:(first + count) * C, t],
+                plane_bf[g, t][:].indirect(offsets[:, first * LCOLS:(first + count) * LCOLS]),
+                COPY,
+            )
+
         def interleave(engine, dst, src):
             dst4 = dst.rearrange("p (c i) t -> p c t i", i=4)
             src4 = src.rearrange("p t (c i) -> p c t i", i=4)
-            if engine == "S":
-                nc.scalar.copy(out=dst4, in_=src4)
-            else:
-                nc.vector.tensor_copy(out=dst4, in_=src4)
+            copy_on(engine, dst4, src4)
 
-        def group_x(g, first, count, engine):
+        def group_x(g, first, count, engine, t0=0, t1=PACK):
             cols = slice(first * C, (first + count) * C)
-            interleave(engine, x_grouped[g][:, cols, :], picked[g][:, :, cols])
+            interleave(engine, x_grouped[g][:, cols, t0:t1], picked[g][:, t0:t1, cols])
 
         def quant_x(g, first, count):
             cols = slice(first * C, (first + count) * C)
@@ -144,8 +165,8 @@ def tile_routed_moe_kernel(tc, xT, w, gate, offs, out):
                     stop=(g == PASSES - 1),
                 )
 
-        def unload(e, fb):
-            nc.scalar.copy(out=sums[e, fb][:], in_=acc[e, fb][:])
+        def unload(e, fb, engine="S"):
+            copy_on(engine, sums[e, fb][:], acc[e, fb][:])
 
         def scatter(e, fb):
             nc.vector.tensor_tensor(
@@ -170,9 +191,10 @@ def tile_routed_moe_kernel(tc, xT, w, gate, offs, out):
         gather(1, 2, 0, 2)
         quant_w(0, 0, 1)
         group_w(0, 1, "S")
-        gather(1, 3, 0, 2)
+        gather(1, 3, 0, 1)
         group_w(1, 0, "S")
         group_x(1, 0, 1, "S")
+        gather(1, 3, 1, 1)
         quant_w(0, 1, 1)
         quant_x(1, 0, 1)
         multiply(0, 0)

@@ -187,21 +187,19 @@ def tile_routed_moe_kernel(tc, xT, w, gate, offs, out):
         group_x(0, 0, 2, "S")
         gather(1, 1, 0, 2)
         group_w(0, 0, "S")
-        quant_x(0, 0, 1)
+        quant_x(0, 0, 2)
         gather(1, 2, 0, 2)
-        quant_w(0, 0, 1)
         group_w(0, 1, "S")
         gather(1, 3, 0, 1)
         group_w(1, 0, "S")
         group_x(1, 0, 1, "S")
         gather(1, 3, 1, 1)
-        quant_w(0, 1, 1)
+        quant_w(0, 0, 2)
         quant_x(1, 0, 1)
         multiply(0, 0)
         multiply(0, 1)
         group_x(1, 1, 1, "S")
-        quant_x(0, 1, 1)
-        unload(0, 0)
+        unload(0, 0, "V")
         quant_w(1, 0, 1)
         quant_x(1, 1, 1)
         group_w(1, 1, "S")

@@ -119,6 +119,22 @@ def tile_routed_moe_kernel(tc, xT, w, gate, offs, out):
             cols = slice(first * C, (first + count) * C)
             interleave(engine, x_grouped[g][:, cols, t0:t1], picked[g][:, t0:t1, cols])
 
+        def group_x_plain(g, first, count, engine, t0=0, t1=PACK):
+            cols = slice(first * C, (first + count) * C)
+            copy_on(engine, x_grouped[g][:, cols, t0:t1], picked[g][:, t0:t1, cols].rearrange("p t n -> p n t"))
+
+        def group_w_plain(e, g, engine):
+            copy_on(engine, w_grouped[e][:, g, :, :], w_raw[e, g][:].rearrange("p j n -> p n j"))
+
+        def late_sums(e, fb, slot):
+            sums[e, fb] = keep.tile([P, C], F32, name=slot)
+
+        def gather_b(g, t, first, count):
+            nc.vector.tensor_copy(
+                x_grouped[g][:, first * C:(first + count) * C, t],
+                plane[g, t][:].indirect(offsets[:, first * LCOLS:(first + count) * LCOLS]),
+            )
+
         def quant_x(g, first, count):
             cols = slice(first * C, (first + count) * C)
             nc.vector.quantize_mx(
@@ -138,7 +154,8 @@ def tile_routed_moe_kernel(tc, xT, w, gate, offs, out):
             w_scales[e] = keep.tile([P, PASSES * N], U8, name="wscales%d" % e, align_bytes=64)
             for fb in range(FB):
                 acc[e, fb] = psum.tile([P, C], F32, name="acc%d%d" % (e, fb))
-                sums[e, fb] = keep.tile([P, C], F32, name="sums%d%d" % (e, fb))
+                if (e, fb) != (0, 1):
+                    sums[e, fb] = keep.tile([P, C], F32, name="sums%d%d" % (e, fb))
 
         def group_w(e, g, engine):
             interleave(engine, w_grouped[e][:, g, :, :], w_raw[e, g][:])
@@ -188,22 +205,24 @@ def tile_routed_moe_kernel(tc, xT, w, gate, offs, out):
         gather(1, 1, 0, 2)
         group_w(0, 0, "S")
         quant_x(0, 0, 2)
-        gather(1, 2, 0, 2)
+        gather(1, 2, 0, 1)
+        gather_b(1, 2, 1, 1)
+        group_x(1, 1, 1, "S", 0, 2)
         group_w(0, 1, "S")
         gather(1, 3, 0, 1)
         group_w(1, 0, "S")
         group_x(1, 0, 1, "S")
-        gather(1, 3, 1, 1)
+        gather_b(1, 3, 1, 1)
         quant_w(0, 0, 2)
         quant_x(1, 0, 1)
         multiply(0, 0)
         multiply(0, 1)
-        group_x(1, 1, 1, "S")
         unload(0, 0, "V")
-        quant_w(1, 0, 1)
         quant_x(1, 1, 1)
+        quant_w(1, 0, 1)
         group_w(1, 1, "S")
         scatter(0, 0)
+        late_sums(0, 1, "wraw11")
         unload(0, 1)
         quant_w(1, 1, 1)
         scatter(0, 1)

@@ -11,14 +11,17 @@ U32 = mybir.dt.uint32
 U16 = mybir.dt.uint16
 U8 = mybir.dt.uint8
 FP8X4 = mybir.dt.float8_e4m3fn_x4
-MULT = mybir.AluOpType.mult
-COPY = mybir.ActivationFunctionType.Copy
 
 P = 128
 PACK = 4
 PASSES = K // (P * PACK)
-FB = N // P
-LCOLS = C // 16
+FEATURE_BLOCKS = N // P
+OFFSETS_A_COLUMN = 16
+LIST_COLUMNS = C // OFFSETS_A_COLUMN
+MX_ALIGN = 64
+RUN = 4
+HALF = PACK // 2
+HELD_BACK = (0, 1)
 
 
 def tile_routed_moe_kernel(tc, xT, w, gate, offs, out):
@@ -28,22 +31,17 @@ def tile_routed_moe_kernel(tc, xT, w, gate, offs, out):
         keep = ctx.enter_context(tc.tile_pool(name="keep", bufs=1))
         psum = ctx.enter_context(tc.psum_pool(name="psum", bufs=1))
 
-        offsets = lists.tile([P, E * C // 16], U16, name="offsets")
+        offsets = lists.tile([P, E * LIST_COLUMNS], U16, name="offsets")
         nc.sync.dma_start(offsets[:], offs)
 
         x_view = xT.rearrange("(g p t) n -> g p t n", p=P, t=PACK)
-        w_view = w.rearrange("e (g p j) n -> e g p j n", p=P, j=PACK)
+        w_view = w.rearrange("e (g p t) n -> e g p t n", p=P, t=PACK)
 
         plane = {}
-        plane_bf = {}
         w_raw = {}
         gate_sb = {}
 
-        def load_x(g, t):
-            plane[g, t] = keep.tile([P, 2 * T], F32, name="plane%d%d" % (g, t))
-            nc.sync.dma_start(out=plane[g, t][:, 0:T], in_=x_view[g, :, t, :])
-
-        def load_xb(g, t):
+        def load_plane(g, t):
             plane[g, t] = keep.tile([P, T], F32, name="plane%d%d" % (g, t))
             nc.sync.dma_start(out=plane[g, t][:], in_=x_view[g, :, t, :])
 
@@ -55,23 +53,21 @@ def tile_routed_moe_kernel(tc, xT, w, gate, offs, out):
             gate_sb[fb] = keep.tile([P, E * C], F32, name="gate%d" % fb)
             nc.sync.dma_start(out=gate_sb[fb][:], in_=gate[fb * P:(fb + 1) * P, :])
 
-        load_x(0, 0)
-        load_x(0, 1)
-        load_x(0, 2)
-        load_x(0, 3)
-        load_x(1, 0)
-        load_x(1, 1)
+        for t in range(PACK):
+            load_plane(0, t)
+        load_plane(1, 0)
+        load_plane(1, 1)
         load_w(0, 0)
-        load_x(1, 2)
+        load_plane(1, 2)
         load_w(0, 1)
-        load_x(1, 3)
+        load_plane(1, 3)
         load_w(1, 0)
         load_gate(0)
         load_w(1, 1)
         load_gate(1)
 
         window = {}
-        for fb in range(FB):
+        for fb in range(FEATURE_BLOCKS):
             window[fb] = keep.tile([P, T], F32, name="window%d" % fb)
             nc.vector.memset(window[fb][:], 0.0)
 
@@ -81,67 +77,9 @@ def tile_routed_moe_kernel(tc, xT, w, gate, offs, out):
         x_scales = {}
         for g in range(PASSES):
             picked[g] = keep.tile([P, PACK, E * C], F32, name="picked%d" % g)
-            x_grouped[g] = keep.tile([P, E * C, PACK], BF16, name="xgrp%d" % g, align_bytes=64)
-            x_codes[g] = keep.tile([P, E * C], U32, name="xcodes%d" % g, align_bytes=64)
-            x_scales[g] = keep.tile([P, E * C], U8, name="xscales%d" % g, align_bytes=64)
-
-        def copy_on(engine, dst, src):
-            if engine == "S":
-                nc.scalar.copy(out=dst, in_=src)
-            elif engine == "G":
-                nc.gpsimd.tensor_copy(out=dst, in_=src)
-            else:
-                nc.vector.tensor_copy(out=dst, in_=src)
-
-        def gather(g, t, first, count):
-            nc.vector.tensor_copy(
-                picked[g][:, t, first * C:(first + count) * C],
-                plane[g, t][:].indirect(offsets[:, first * LCOLS:(first + count) * LCOLS]),
-            )
-
-        def cast_plane(g, t, engine):
-            plane_bf[g, t] = keep.tile([P, T], BF16, name="planebf%d%d" % (g, t))
-            copy_on(engine, plane_bf[g, t][:], plane[g, t][:])
-
-        def gather_s(g, t, first, count):
-            nc.scalar.activation(
-                x_grouped[g][:, first * C:(first + count) * C, t],
-                plane_bf[g, t][:].indirect(offsets[:, first * LCOLS:(first + count) * LCOLS]),
-                COPY,
-            )
-
-        def interleave(engine, dst, src):
-            dst4 = dst.rearrange("p (c i) t -> p c t i", i=4)
-            src4 = src.rearrange("p t (c i) -> p c t i", i=4)
-            copy_on(engine, dst4, src4)
-
-        def group_x(g, first, count, engine, t0=0, t1=PACK):
-            cols = slice(first * C, (first + count) * C)
-            interleave(engine, x_grouped[g][:, cols, t0:t1], picked[g][:, t0:t1, cols])
-
-        def group_x_plain(g, first, count, engine, t0=0, t1=PACK):
-            cols = slice(first * C, (first + count) * C)
-            copy_on(engine, x_grouped[g][:, cols, t0:t1], picked[g][:, t0:t1, cols].rearrange("p t n -> p n t"))
-
-        def group_w_plain(e, g, engine):
-            copy_on(engine, w_grouped[e][:, g, :, :], w_raw[e, g][:].rearrange("p j n -> p n j"))
-
-        def late_sums(e, fb, slot):
-            sums[e, fb] = keep.tile([P, C], F32, name=slot)
-
-        def gather_b(g, t, first, count):
-            nc.vector.tensor_copy(
-                x_grouped[g][:, first * C:(first + count) * C, t],
-                plane[g, t][:].indirect(offsets[:, first * LCOLS:(first + count) * LCOLS]),
-            )
-
-        def quant_x(g, first, count):
-            cols = slice(first * C, (first + count) * C)
-            nc.vector.quantize_mx(
-                out=x_codes[g][:, cols].bitcast(FP8X4),
-                scales=x_scales[g][:, cols],
-                in_=x_grouped[g][:, cols, :].rearrange("p n t -> p (n t)"),
-            )
+            x_grouped[g] = keep.tile([P, E * C, PACK], BF16, name="xgrp%d" % g, align_bytes=MX_ALIGN)
+            x_codes[g] = keep.tile([P, E * C], U32, name="xcodes%d" % g, align_bytes=MX_ALIGN)
+            x_scales[g] = keep.tile([P, E * C], U8, name="xscales%d" % g, align_bytes=MX_ALIGN)
 
         w_grouped = {}
         w_codes = {}
@@ -149,87 +87,117 @@ def tile_routed_moe_kernel(tc, xT, w, gate, offs, out):
         acc = {}
         sums = {}
         for e in range(E):
-            w_grouped[e] = keep.tile([P, PASSES, N, PACK], BF16, name="wgrp%d" % e, align_bytes=64)
-            w_codes[e] = keep.tile([P, PASSES * N], U32, name="wcodes%d" % e, align_bytes=64)
-            w_scales[e] = keep.tile([P, PASSES * N], U8, name="wscales%d" % e, align_bytes=64)
-            for fb in range(FB):
+            w_grouped[e] = keep.tile([P, PASSES, N, PACK], BF16, name="wgrp%d" % e, align_bytes=MX_ALIGN)
+            w_codes[e] = keep.tile([P, PASSES * N], U32, name="wcodes%d" % e, align_bytes=MX_ALIGN)
+            w_scales[e] = keep.tile([P, PASSES * N], U8, name="wscales%d" % e, align_bytes=MX_ALIGN)
+            for fb in range(FEATURE_BLOCKS):
                 acc[e, fb] = psum.tile([P, C], F32, name="acc%d%d" % (e, fb))
-                if (e, fb) != (0, 1):
+                if (e, fb) != HELD_BACK:
                     sums[e, fb] = keep.tile([P, C], F32, name="sums%d%d" % (e, fb))
 
-        def group_w(e, g, engine):
-            interleave(engine, w_grouped[e][:, g, :, :], w_raw[e, g][:])
+        def slots_of(first, count):
+            return slice(first * C, (first + count) * C)
+
+        def gather(g, t, first, count):
+            nc.vector.tensor_copy(
+                picked[g][:, t, slots_of(first, count)],
+                plane[g, t][:].indirect(offsets[:, first * LIST_COLUMNS:(first + count) * LIST_COLUMNS]),
+            )
+
+        def gather_interleaved(g, t, e):
+            nc.vector.tensor_copy(
+                x_grouped[g][:, slots_of(e, 1), t],
+                plane[g, t][:].indirect(offsets[:, e * LIST_COLUMNS:(e + 1) * LIST_COLUMNS]),
+            )
+
+        def interleave(dst, src):
+            nc.scalar.copy(
+                out=dst.rearrange("p (c i) t -> p c t i", i=RUN),
+                in_=src.rearrange("p t (c i) -> p c t i", i=RUN),
+            )
+
+        def group_x(g, first, count, places=PACK):
+            cols = slots_of(first, count)
+            interleave(x_grouped[g][:, cols, 0:places], picked[g][:, 0:places, cols])
+
+        def quant_x(g, first, count):
+            cols = slots_of(first, count)
+            nc.vector.quantize_mx(
+                out=x_codes[g][:, cols].bitcast(FP8X4),
+                scales=x_scales[g][:, cols],
+                in_=x_grouped[g][:, cols, :].rearrange("p n t -> p (n t)"),
+            )
+
+        def group_w(e, g):
+            interleave(w_grouped[e][:, g, :, :], w_raw[e, g][:])
 
         def quant_w(e, first, count):
             cols = slice(first * N, (first + count) * N)
             nc.vector.quantize_mx(
                 out=w_codes[e][:, cols].bitcast(FP8X4),
                 scales=w_scales[e][:, cols],
-                in_=w_grouped[e][:, first:first + count, :, :].rearrange("p g n j -> p (g n j)"),
+                in_=w_grouped[e][:, first:first + count, :, :].rearrange("p g n t -> p (g n t)"),
             )
 
         def multiply(e, fb):
             for g in range(PASSES):
-                wcols = slice(g * N + fb * P, g * N + (fb + 1) * P)
-                xcols = slice(e * C, (e + 1) * C)
+                w_cols = slice(g * N + fb * P, g * N + (fb + 1) * P)
+                x_cols = slots_of(e, 1)
                 nc.tensor.matmul_mx(
                     out=acc[e, fb][:],
-                    lhsT=w_codes[e][:, wcols].bitcast(FP8X4),
-                    lhsT_scale=w_scales[e][:, wcols],
-                    rhs=x_codes[g][:, xcols].bitcast(FP8X4),
-                    rhs_scale=x_scales[g][:, xcols],
+                    lhsT=w_codes[e][:, w_cols].bitcast(FP8X4),
+                    lhsT_scale=w_scales[e][:, w_cols],
+                    rhs=x_codes[g][:, x_cols].bitcast(FP8X4),
+                    rhs_scale=x_scales[g][:, x_cols],
                     start=(g == 0),
                     stop=(g == PASSES - 1),
                 )
 
-        def unload(e, fb, engine="S"):
-            copy_on(engine, sums[e, fb][:], acc[e, fb][:])
-
         def scatter(e, fb):
             nc.vector.tensor_tensor(
-                window[fb][:].indirect(offsets[:, e * LCOLS:(e + 1) * LCOLS]),
+                window[fb][:].indirect(offsets[:, e * LIST_COLUMNS:(e + 1) * LIST_COLUMNS]),
                 sums[e, fb][:],
-                gate_sb[fb][:, e * C:(e + 1) * C],
-                MULT,
+                gate_sb[fb][:, slots_of(e, 1)],
+                mybir.AluOpType.mult,
             )
 
         def store(fb):
             nc.sync.dma_start(out=out[fb * P:(fb + 1) * P, :], in_=window[fb][:])
 
-        gather(0, 0, 0, 2)
-        gather(0, 1, 0, 2)
-        gather(0, 2, 0, 2)
-        gather(0, 3, 0, 2)
-        gather(1, 0, 0, 2)
-        group_x(0, 0, 2, "S")
-        gather(1, 1, 0, 2)
-        group_w(0, 0, "S")
-        quant_x(0, 0, 2)
+        gather(0, 0, 0, E)
+        gather(0, 1, 0, E)
+        gather(0, 2, 0, E)
+        gather(0, 3, 0, E)
+        gather(1, 0, 0, E)
+        group_x(0, 0, E)
+        gather(1, 1, 0, E)
+        group_w(0, 0)
+        quant_x(0, 0, E)
         gather(1, 2, 0, 1)
-        gather_b(1, 2, 1, 1)
-        group_x(1, 1, 1, "S", 0, 2)
-        group_w(0, 1, "S")
+        gather_interleaved(1, 2, 1)
+        group_x(1, 1, 1, HALF)
+        group_w(0, 1)
         gather(1, 3, 0, 1)
-        group_w(1, 0, "S")
-        group_x(1, 0, 1, "S")
-        gather_b(1, 3, 1, 1)
-        quant_w(0, 0, 2)
+        group_w(1, 0)
+        group_x(1, 0, 1)
+        gather_interleaved(1, 3, 1)
+        quant_w(0, 0, PASSES)
         quant_x(1, 0, 1)
         multiply(0, 0)
         multiply(0, 1)
-        unload(0, 0, "V")
+        nc.vector.tensor_copy(out=sums[0, 0][:], in_=acc[0, 0][:])
         quant_x(1, 1, 1)
         quant_w(1, 0, 1)
-        group_w(1, 1, "S")
+        group_w(1, 1)
         scatter(0, 0)
-        late_sums(0, 1, "wraw11")
-        unload(0, 1)
+        sums[HELD_BACK] = keep.tile([P, C], F32, name="wraw11")
+        nc.scalar.copy(out=sums[0, 1][:], in_=acc[0, 1][:])
         quant_w(1, 1, 1)
         scatter(0, 1)
         multiply(1, 0)
-        unload(1, 0)
+        nc.scalar.copy(out=sums[1, 0][:], in_=acc[1, 0][:])
         multiply(1, 1)
-        unload(1, 1)
+        nc.scalar.copy(out=sums[1, 1][:], in_=acc[1, 1][:])
         scatter(1, 0)
         store(0)
         scatter(1, 1)

from contextlib import ExitStack

import concourse.mybir as mybir

K, T, E, C, N = 1024, 1024, 2, 256, 256
FLOPS = 2 * K * N * E * C

F32 = mybir.dt.float32
BF16 = mybir.dt.bfloat16
U32 = mybir.dt.uint32
U16 = mybir.dt.uint16
U8 = mybir.dt.uint8
FP8X4 = mybir.dt.float8_e4m3fn_x4

P = 128
PACK = 4
PASSES = K // (P * PACK)
FEATURE_BLOCKS = N // P
OFFSETS_A_COLUMN = 16
LIST_COLUMNS = C // OFFSETS_A_COLUMN
MX_ALIGN = 64
RUN = 4
HALF = PACK // 2
HELD_BACK = (0, 1)


def tile_routed_moe_kernel(tc, xT, w, gate, offs, out):
    nc = tc.nc
    with ExitStack() as ctx:
        lists = ctx.enter_context(tc.tile_pool(name="lists", bufs=1))
        keep = ctx.enter_context(tc.tile_pool(name="keep", bufs=1))
        psum = ctx.enter_context(tc.psum_pool(name="psum", bufs=1))

        offsets = lists.tile([P, E * LIST_COLUMNS], U16, name="offsets")
        nc.sync.dma_start(offsets[:], offs)

        x_view = xT.rearrange("(g p t) n -> g p t n", p=P, t=PACK)
        w_view = w.rearrange("e (g p t) n -> e g p t n", p=P, t=PACK)

        plane = {}
        w_raw = {}
        gate_sb = {}

        def load_plane(g, t):
            plane[g, t] = keep.tile([P, T], F32, name="plane%d%d" % (g, t))
            nc.sync.dma_start(out=plane[g, t][:], in_=x_view[g, :, t, :])

        def load_w(e, g):
            w_raw[e, g] = keep.tile([P, PACK, N], F32, name="wraw%d%d" % (e, g))
            nc.sync.dma_start(out=w_raw[e, g][:], in_=w_view[e, g])

        def load_gate(fb):
            gate_sb[fb] = keep.tile([P, E * C], F32, name="gate%d" % fb)
            nc.sync.dma_start(out=gate_sb[fb][:], in_=gate[fb * P:(fb + 1) * P, :])

        for t in range(PACK):
            load_plane(0, t)
        load_plane(1, 0)
        load_plane(1, 1)
        load_w(0, 0)
        load_plane(1, 2)
        load_w(0, 1)
        load_plane(1, 3)
        load_w(1, 0)
        load_gate(0)
        load_w(1, 1)
        load_gate(1)

        window = {}
        for fb in range(FEATURE_BLOCKS):
            window[fb] = keep.tile([P, T], F32, name="window%d" % fb)
            nc.vector.memset(window[fb][:], 0.0)

        picked = {}
        x_grouped = {}
        x_codes = {}
        x_scales = {}
        for g in range(PASSES):
            picked[g] = keep.tile([P, PACK, E * C], F32, name="picked%d" % g)
            x_grouped[g] = keep.tile([P, E * C, PACK], BF16, name="xgrp%d" % g, align_bytes=MX_ALIGN)
            x_codes[g] = keep.tile([P, E * C], U32, name="xcodes%d" % g, align_bytes=MX_ALIGN)
            x_scales[g] = keep.tile([P, E * C], U8, name="xscales%d" % g, align_bytes=MX_ALIGN)

        w_grouped = {}
        w_codes = {}
        w_scales = {}
        acc = {}
        sums = {}
        for e in range(E):
            w_grouped[e] = keep.tile([P, PASSES, N, PACK], BF16, name="wgrp%d" % e, align_bytes=MX_ALIGN)
            w_codes[e] = keep.tile([P, PASSES * N], U32, name="wcodes%d" % e, align_bytes=MX_ALIGN)
            w_scales[e] = keep.tile([P, PASSES * N], U8, name="wscales%d" % e, align_bytes=MX_ALIGN)
            for fb in range(FEATURE_BLOCKS):
                acc[e, fb] = psum.tile([P, C], F32, name="acc%d%d" % (e, fb))
                if (e, fb) != HELD_BACK:
                    sums[e, fb] = keep.tile([P, C], F32, name="sums%d%d" % (e, fb))

        def slots_of(first, count):
            return slice(first * C, (first + count) * C)

        def gather(g, t, first, count):
            nc.vector.tensor_copy(
                picked[g][:, t, slots_of(first, count)],
                plane[g, t][:].indirect(offsets[:, first * LIST_COLUMNS:(first + count) * LIST_COLUMNS]),
            )

        def gather_interleaved(g, t, e):
            nc.vector.tensor_copy(
                x_grouped[g][:, slots_of(e, 1), t],
                plane[g, t][:].indirect(offsets[:, e * LIST_COLUMNS:(e + 1) * LIST_COLUMNS]),
            )

        def interleave(dst, src):
            nc.scalar.copy(
                out=dst.rearrange("p (c i) t -> p c t i", i=RUN),
                in_=src.rearrange("p t (c i) -> p c t i", i=RUN),
            )

        def group_x(g, first, count, places=PACK):
            cols = slots_of(first, count)
            interleave(x_grouped[g][:, cols, 0:places], picked[g][:, 0:places, cols])

        def quant_x(g, first, count):
            cols = slots_of(first, count)
            nc.vector.quantize_mx(
                out=x_codes[g][:, cols].bitcast(FP8X4),
                scales=x_scales[g][:, cols],
                in_=x_grouped[g][:, cols, :].rearrange("p n t -> p (n t)"),
            )

        def group_w(e, g):
            interleave(w_grouped[e][:, g, :, :], w_raw[e, g][:])

        def quant_w(e, first, count):
            cols = slice(first * N, (first + count) * N)
            nc.vector.quantize_mx(
                out=w_codes[e][:, cols].bitcast(FP8X4),
                scales=w_scales[e][:, cols],
                in_=w_grouped[e][:, first:first + count, :, :].rearrange("p g n t -> p (g n t)"),
            )

        def multiply(e, fb):
            for g in range(PASSES):
                w_cols = slice(g * N + fb * P, g * N + (fb + 1) * P)
                x_cols = slots_of(e, 1)
                nc.tensor.matmul_mx(
                    out=acc[e, fb][:],
                    lhsT=w_codes[e][:, w_cols].bitcast(FP8X4),
                    lhsT_scale=w_scales[e][:, w_cols],
                    rhs=x_codes[g][:, x_cols].bitcast(FP8X4),
                    rhs_scale=x_scales[g][:, x_cols],
                    start=(g == 0),
                    stop=(g == PASSES - 1),
                )

        def scatter(e, fb):
            nc.vector.tensor_tensor(
                window[fb][:].indirect(offsets[:, e * LIST_COLUMNS:(e + 1) * LIST_COLUMNS]),
                sums[e, fb][:],
                gate_sb[fb][:, slots_of(e, 1)],
                mybir.AluOpType.mult,
            )

        def store(fb):
            nc.sync.dma_start(out=out[fb * P:(fb + 1) * P, :], in_=window[fb][:])

        gather(0, 0, 0, E)
        gather(0, 1, 0, E)
        gather(0, 2, 0, E)
        gather(0, 3, 0, E)
        gather(1, 0, 0, E)
        group_x(0, 0, E)
        gather(1, 1, 0, E)
        group_w(0, 0)
        quant_x(0, 0, E)
        gather(1, 2, 0, 1)
        gather_interleaved(1, 2, 1)
        group_x(1, 1, 1, HALF)
        group_w(0, 1)
        gather(1, 3, 0, 1)
        group_w(1, 0)
        group_x(1, 0, 1)
        gather_interleaved(1, 3, 1)
        quant_w(0, 0, PASSES)
        quant_x(1, 0, 1)
        multiply(0, 0)
        multiply(0, 1)
        nc.vector.tensor_copy(out=sums[0, 0][:], in_=acc[0, 0][:])
        quant_x(1, 1, 1)
        quant_w(1, 0, 1)
        group_w(1, 1)
        scatter(0, 0)
        sums[HELD_BACK] = keep.tile([P, C], F32, name="wraw11")
        nc.scalar.copy(out=sums[0, 1][:], in_=acc[0, 1][:])
        quant_w(1, 1, 1)
        scatter(0, 1)
        multiply(1, 0)
        nc.scalar.copy(out=sums[1, 0][:], in_=acc[1, 0][:])
        multiply(1, 1)
        nc.scalar.copy(out=sums[1, 1][:], in_=acc[1, 1][:])
        scatter(1, 0)
        store(0)
        scatter(1, 1)
        store(1)
